import numpy as np
import ml_dtypes


def mxq(x, axis, fmt="e4m3"):
    dtype, down = {"e4m3": (ml_dtypes.float8_e4m3fn, 7), "e5m2": (ml_dtypes.float8_e5m2, 14)}[fmt]
    v = np.moveaxis(np.asarray(x, np.float32).astype(ml_dtypes.bfloat16).astype(np.float64), axis, -1)
    blocks = v.reshape(v.shape[:-1] + (-1, 32))
    amax = np.abs(blocks).max(-1, keepdims=True)
    byte = np.maximum(np.where(amax > 0, np.frexp(amax)[1] - 1 + 127, 0) - down, 1)
    scale = np.exp2(byte - 127.0)
    codes = (blocks / scale).astype(np.float32).astype(dtype).astype(np.float64)
    return np.moveaxis((codes * scale).reshape(v.shape), -1, axis)


WIDE = False


def mx_kscale(k):
    if not WIDE:
        return np.ones(k)
    levels = np.array([10, -10, 5, -5, 0])
    if k % 512:
        return np.exp2(np.random.permutation(np.resize(levels, k // 32))).repeat(32)
    a = np.empty((k // 512, 16))
    for p in range(k // 512):
        a[p, :8] = np.random.permutation(np.resize(levels, 8))
        for g in range(8):
            far = levels[np.abs(levels - a[p, g]) >= 10]
            a[p, g + 8] = far[np.random.randint(len(far))]
    return np.exp2(a.ravel()).repeat(32)


def f64(x):
    return np.asarray(x).astype(np.float64)


def striped(idx):
    return np.tile(idx.reshape(-1, 16).T, (8, 1)).astype(np.uint16)


def unstriped(offs):
    return offs[:16].T.reshape(-1).astype(np.int64)


def gelu(v):
    return 0.5 * v * (1.0 + np.tanh(np.sqrt(2.0 / np.pi) * (v + 0.044715 * v**3)))


K, T, D, V, H, N = 2048, 512, 6, 256, 1024, 256
P = 2 ** 7


def setup_inputs():
    n = np.random.standard_normal
    s = mx_kscale(K)[:, None]
    u = mx_kscale(H)
    return {
        "xT": (n((K, T)) * s).astype(np.float32),
        "w1": (n((K, H)) / np.sqrt(K) / s * u).astype(np.float32),
        "w2": (n((H, N)) / np.sqrt(H) / u[:, None]).astype(np.float32),
        "gate": np.tile(np.random.uniform(0.2, 1.0, (D, 1, V)) / np.sqrt(D), (1, P, 1)).astype(np.float32),
        "pos1": striped(np.random.permutation(T)[:V]),
        "pos2": striped(np.random.permutation(T)[:V]),
        "pos3": striped(np.random.permutation(T)[:V]),
        "pos4": striped(np.random.permutation(T)[:V]),
        "pos5": striped(np.random.permutation(T)[:V]),
        "pos6": striped(np.random.permutation(T)[:V]),
    }


def reference(xT, w1, w2, gate, pos1, pos2, pos3, pos4, pos5, pos6):
    h = gelu(mxq(f64(w1), 0, "e4m3").T @ mxq(f64(xT), 0, "e4m3"))
    z = sum(f64(gate)[d, :1] * h[:, unstriped(p)] for d, p in enumerate((pos1, pos2, pos3, pos4, pos5, pos6)))
    return mxq(f64(w2), 0, "e4m3").T @ mxq(z, 0, "e4m3")

@@ -1,0 +1,265 @@
+import concourse.mybir as mybir
+from concourse.masks import make_identity
+
+K, T, D, V, H, N = 2048, 512, 6, 256, 1024, 256
+
+F32 = mybir.dt.float32
+BF16 = mybir.dt.bfloat16
+U32 = mybir.dt.uint32
+U8 = mybir.dt.uint8
+U16 = mybir.dt.uint16
+FP8X4 = mybir.dt.float8_e4m3fn_x4
+MULT = mybir.AluOpType.mult
+GELU = mybir.ActivationFunctionType.Gelu_apprx_tanh
+
+FLOPS = 2 * K * H * T + 2 * D * H * V + 2 * H * N * V
+
+P = 128
+PACK = 4
+PASS = P * PACK
+C = K // PASS
+Q = H // PASS
+HALF = V // 2
+CHUNKS = (128, 128, 256, 256, 256)
+X_VECTOR = 320
+
+
+def tile_picked_gcn_mlp_gelu_sub_l_kernel(
+    tc, xT, w1, w2, gate, pos1, pos2, pos3, pos4, pos5, pos6, out
+):
+    nc = tc.nc
+    lists_dram = (pos1, pos2, pos3, pos4, pos5, pos6)
+    with (
+        tc.tile_pool(name="held", bufs=1) as held,
+        tc.tile_pool(name="wraw", bufs=3) as wraw,
+        tc.tile_pool(name="stage", bufs=2) as stage,
+        tc.psum_pool(name="ps_h", bufs=2) as ps_h,
+        tc.psum_pool(name="ps_z", bufs=1) as ps_z,
+    ):
+        warm_in = held.tile([P, 1], F32)
+        warm_out = held.tile([P, 1], F32)
+        nc.vector.memset(warm_in[:], 0.0)
+        nc.scalar.activation(warm_out[:], warm_in[:], GELU)
+        ident = held.tile([P, P], F32)
+        make_identity(nc, ident[:])
+
+        starts = [sum(CHUNKS[:n]) for n in range(len(CHUNKS))]
+        w_raw = {}
+
+        def load_chunk(n):
+            raw = wraw.tile([P, C, PACK, CHUNKS[n]], F32, name=f"w_raw{CHUNKS[n]}")
+            for c in range(C):
+                nc.sync.dma_start(
+                    out=raw[:, c],
+                    in_=w1[c * PASS : (c + 1) * PASS, starts[n] : starts[n] + CHUNKS[n]].rearrange(
+                        "(p j) w -> p j w", j=PACK
+                    ),
+                )
+            w_raw[n] = raw
+
+        load_chunk(0)
+        x_pieces = [(c, 0, T) for c in range(C - 1)] + [(C - 1, 0, T // 2), (C - 1, T // 2, T // 2)]
+        x_raw = []
+        lists = []
+        for n, (c, t0, width) in enumerate(x_pieces):
+            raw = held.tile([P, PACK, width], F32, name=f"x_raw{n}")
+            nc.sync.dma_start(
+                out=raw[:],
+                in_=xT[c * PASS : (c + 1) * PASS, t0 : t0 + width].rearrange("(p j) t -> p j t", j=PACK),
+            )
+            x_raw.append(raw)
+            if n == 1:
+                for d in range(D):
+                    lst = held.tile([P, V // 16], U16, name=f"list{d}")
+                    nc.sync.dma_start(lst[:], lists_dram[d])
+                    lists.append(lst)
+        gates = held.tile([P, D, V], F32)
+        nc.sync.dma_start(out=gates[:], in_=gate.rearrange("d p v -> p d v"))
+        load_chunk(1)
+        load_chunk(2)
+        load_chunk(3)
+        w2_raw = held.tile([P, Q, PACK, N], F32)
+        nc.sync.dma_start(out=w2_raw[:], in_=w2.rearrange("(q p j) m -> p q j m", q=Q, j=PACK))
+        load_chunk(4)
+
+        def interleave(copy, dst, src):
+            copy(
+                out=dst.rearrange("p (c i) j -> p c j i", i=4),
+                in_=src.rearrange("p j (c i) -> p c j i", i=4),
+            )
+
+        w_codes, w_scales = [], []
+
+        w_g = {}
+
+        def copy_chunk(n):
+            width = CHUNKS[n]
+            grouped = stage.tile([P, C, width, PACK], BF16, name=f"w_g{width}", align_bytes=64)
+            w_g[n] = grouped
+            return [(grouped[:, c], w_raw[n][:, c]) for c in range(C)]
+
+        def quantize_chunk(n):
+            width = CHUNKS[n]
+            codes = held.tile([P, C, width], U32, name=f"w_codes{n}", align_bytes=64)
+            scales = held.tile([P, C, width], U8, name=f"w_scales{n}", align_bytes=64)
+            nc.vector.quantize_mx(
+                out=codes[:].rearrange("p c w -> p (c w)").bitcast(FP8X4),
+                scales=scales[:].rearrange("p c w -> p (c w)"),
+                in_=w_g[n][:].rearrange("p c w j -> p (c w j)"),
+            )
+            for b in range(width // P):
+                w_codes.append(codes[:, :, b * P : (b + 1) * P])
+                w_scales.append(scales[:, :, b * P : (b + 1) * P])
+
+        for dst, src in copy_chunk(0):
+            interleave(nc.scalar.copy, dst, src)
+        x_codes = held.tile([P, C, T], U32, align_bytes=64)
+        x_scales = held.tile([P, C, T], U8, align_bytes=64)
+        x_g = []
+
+        def copy_x(n):
+            width = x_pieces[n][2]
+            cut = width * 11 // 16
+            grouped = held.tile([P, width, PACK], BF16, name=f"x_g{n}", align_bytes=64)
+            interleave(nc.vector.tensor_copy, grouped[:, :cut], x_raw[n][:, :, :cut])
+            interleave(nc.scalar.copy, grouped[:, cut:], x_raw[n][:, :, cut:])
+            x_g.append(grouped)
+
+        def quantize_x(n):
+            c, t0, width = x_pieces[n]
+            nc.vector.quantize_mx(
+                out=x_codes[:, c, t0 : t0 + width].bitcast(FP8X4),
+                scales=x_scales[:, c, t0 : t0 + width],
+                in_=x_g[n][:].rearrange("p t j -> p (t j)"),
+            )
+
+        copy_x(0)
+        quantize_chunk(0)
+        for n in range(1, len(x_pieces)):
+            copy_x(n)
+            quantize_x(n - 1)
+        quantize_x(len(x_pieces) - 1)
+
+        def project(i, parts=1):
+            acc = ps_h.tile([P, T], F32, name="acc_h")
+            h = stage.tile([P, T], F32, name="h")
+            width = T // parts
+            for part in range(parts):
+                nodes = slice(part * width, (part + 1) * width)
+                for c in range(C):
+                    nc.tensor.matmul_mx(
+                        out=acc[:, nodes],
+                        lhsT=w_codes[i][:, c].bitcast(FP8X4),
+                        lhsT_scale=w_scales[i][:, c],
+                        rhs=x_codes[:, c, nodes].bitcast(FP8X4),
+                        rhs_scale=x_scales[:, c, nodes],
+                        start=(c == 0),
+                        stop=(c == C - 1),
+                    )
+                nc.scalar.activation(h[:, nodes], acc[:, nodes], GELU)
+            return h
+
+        zT = [held.tile([P, Q, PACK, P], F32, name=f"zT{half}") for half in range(2)]
+        z_codes = held.tile([P, Q, V], U32, align_bytes=64)
+        z_scales = held.tile([P, Q, V], U8, align_bytes=64)
+
+        def gather(h, d):
+            prod = stage.tile([P, V], F32, name=f"prod{d}")
+            nc.vector.tensor_tensor(prod[:], h[:].indirect(lists[d][:]), gates[:, d], MULT)
+            return prod
+
+        def add_up(i, prods):
+            q, b = divmod(i, PACK)
+            accs = [ps_z.tile([P, P], F32, name=f"acc_z{half}") for half in range(2)]
+            for d in range(D):
+                for half in range(2):
+                    nc.tensor.matmul(
+                        accs[half][:],
+                        lhsT=prods[d][:, half * HALF : (half + 1) * HALF],
+                        rhs=ident[:],
+                        start=(d == 0),
+                        stop=(d == D - 1),
+                        is_transpose=True,
+                    )
+            for half in range(2):
+                copy = nc.vector.tensor_copy if (half and i == H // P - 1) else nc.scalar.copy
+                copy(
+                    out=zT[half][:, q, :, 32 * b : 32 * (b + 1)],
+                    in_=accs[half][:].rearrange("p (m t) -> p t m", t=PACK),
+                )
+
+        def turn_back(q):
+            grouped = stage.tile([P, V, PACK], BF16, name="z_g", align_bytes=64)
+            for half in range(2):
+                back = ps_z.tile([P, PACK, HALF], F32, name=f"back{half}")
+                for t in range(PACK):
+                    nc.tensor.transpose(back[:, t], zT[half][:, q, t], ident[:])
+                copy = nc.vector.tensor_copy if (half and q) else nc.scalar.copy
+                copy(out=grouped[:, half * HALF : (half + 1) * HALF], in_=back[:].rearrange("p t v -> p v t"))
+            return grouped
+
+        def quantize_z(q, grouped):
+            nc.vector.quantize_mx(
+                out=z_codes[:, q].bitcast(FP8X4),
+                scales=z_scales[:, q],
+                in_=grouped[:].rearrange("p v t -> p (v t)"),
+            )
+
+        h_next = project(0, parts=2)
+        for dst, src in copy_chunk(1):
+            interleave(nc.scalar.copy, dst, src)
+        n_tiles = H // P
+        w2_g = held.tile([P, Q, N, PACK], BF16, align_bytes=64)
+        w2_codes = held.tile([P, Q, N], U32, align_bytes=64)
+        w2_scales = held.tile([P, Q, N], U8, align_bytes=64)
+        background = copy_chunk(2) + copy_chunk(3) + [(w2_g[:, q], w2_raw[:, q]) for q in range(Q)]
+        pending = None
+        for i in range(n_tiles):
+            h = h_next
+            prods = []
+            for d in range(D):
+                if (i, d) == (0, 4):
+                    quantize_chunk(1)
+                if (i, d) == (1, 4):
+                    quantize_chunk(2)
+                if (i, d) == (1, 5):
+                    background += copy_chunk(4)
+                if (i, d) == (3, 1):
+                    quantize_chunk(3)
+                if (i, d) == (5, 1):
+                    quantize_chunk(4)
+                if (i, d) == (5, 3):
+                    quantize_z(0, pending)
+                if (i, d) == (6, 0):
+                    nc.vector.quantize_mx(
+                        out=w2_codes[:].rearrange("p q m -> p (q m)").bitcast(FP8X4),
+                        scales=w2_scales[:].rearrange("p q m -> p (q m)"),
+                        in_=w2_g[:].rearrange("p q m j -> p (q m j)"),
+                    )
+                prods.append(gather(h, d))
+                if d == 4 and i + 1 < n_tiles:
+                    h_next = project(i + 1)
+                if i * D + d >= 2 and d % 2 == 0 and background:
+                    interleave(nc.scalar.copy, *background.pop(0))
+            add_up(i, prods)
+            if i % PACK == PACK - 1:
+                pending = turn_back(i // PACK)
+        quantize_z(1, pending)
+        for b in range(N // P):
+            acc = ps_z.tile([P, V], F32, name=f"acc_o{b}")
+            for q in range(Q):
+                nc.tensor.matmul_mx(
+                    out=acc[:],
+                    lhsT=w2_codes[:, q, b * P : (b + 1) * P].bitcast(FP8X4),
+                    lhsT_scale=w2_scales[:, q, b * P : (b + 1) * P],
+                    rhs=z_codes[:, q].bitcast(FP8X4),
+                    rhs_scale=z_scales[:, q],
+                    start=(q == 0),
+                    stop=(q == Q - 1),
+                )
+            res = held.tile([P, V], F32, name=f"res{b}")
+            if b:
+                nc.scalar.copy(out=res[:], in_=acc[:])
+            else:
+                nc.vector.tensor_copy(out=res[:], in_=acc[:])
+            nc.sync.dma_start(out=out[b * P : (b + 1) * P, :], in_=res[:])

@@ -20,8 +20,16 @@ PASS = P * PACK
 C = K // PASS
 Q = H // PASS
 HALF = V // 2
-CHUNKS = (128, 128, 256, 256, 256)
-X_VECTOR = 320
+CHUNKS = (256, 256, 256, 256)
+COPY_SLOTS = (1, 2, 4, 6, 8, 9, 11, 13, 15, 16, 18, 20, 24, 27)
+QUANT_SLOTS = (8, 18, 28)
+PROJECT_SLOTS = (2, 10, 14, 20, 26, 30, 38)
+X_CUT = 11
+Z_SLOT = 33
+W2_SLOT = 40
+W0Q = 0
+GATE_CUT = 6
+PIECES = (512, 512, 512, 256, 256)
 
 
 def tile_picked_gcn_mlp_gelu_sub_l_kernel(
@@ -33,6 +41,7 @@ def tile_picked_gcn_mlp_gelu_sub_l_kernel(
         tc.tile_pool(name="held", bufs=1) as held,
         tc.tile_pool(name="wraw", bufs=3) as wraw,
         tc.tile_pool(name="stage", bufs=2) as stage,
+        tc.tile_pool(name="hpool", bufs=4) as hpool,
         tc.psum_pool(name="ps_h", bufs=2) as ps_h,
         tc.psum_pool(name="ps_z", bufs=1) as ps_z,
     ):
@@ -58,7 +67,7 @@ def tile_picked_gcn_mlp_gelu_sub_l_kernel(
             w_raw[n] = raw
 
         load_chunk(0)
-        x_pieces = [(c, 0, T) for c in range(C - 1)] + [(C - 1, 0, T // 2), (C - 1, T // 2, T // 2)]
+        x_pieces = [(sum(PIECES[:n]) // T, sum(PIECES[:n]) % T, PIECES[n]) for n in range(len(PIECES))]
         x_raw = []
         lists = []
         for n, (c, t0, width) in enumerate(x_pieces):
@@ -74,13 +83,14 @@ def tile_picked_gcn_mlp_gelu_sub_l_kernel(
                     nc.sync.dma_start(lst[:], lists_dram[d])
                     lists.append(lst)
         gates = held.tile([P, D, V], F32)
-        nc.sync.dma_start(out=gates[:], in_=gate.rearrange("d p v -> p d v"))
-        load_chunk(1)
-        load_chunk(2)
-        load_chunk(3)
-        w2_raw = held.tile([P, Q, PACK, N], F32)
-        nc.sync.dma_start(out=w2_raw[:], in_=w2.rearrange("(q p j) m -> p q j m", q=Q, j=PACK))
-        load_chunk(4)
+        nc.sync.dma_start(out=gates[:, :GATE_CUT], in_=gate[:GATE_CUT].rearrange("d p v -> p d v"))
+        for n in range(1, len(CHUNKS)):
+            load_chunk(n)
+            if n == 1 and GATE_CUT < D:
+                nc.sync.dma_start(out=gates[:, GATE_CUT:], in_=gate[GATE_CUT:].rearrange("d p v -> p d v"))
+            if n == len(CHUNKS) - 2:
+                w2_raw = held.tile([P, Q, PACK, N], F32)
+                nc.sync.dma_start(out=w2_raw[:], in_=w2.rearrange("(q p j) m -> p q j m", q=Q, j=PACK))
 
         def interleave(copy, dst, src):
             copy(
@@ -119,7 +129,7 @@ def tile_picked_gcn_mlp_gelu_sub_l_kernel(
 
         def copy_x(n):
             width = x_pieces[n][2]
-            cut = width * 11 // 16
+            cut = width * X_CUT // 16
             grouped = held.tile([P, width, PACK], BF16, name=f"x_g{n}", align_bytes=64)
             interleave(nc.vector.tensor_copy, grouped[:, :cut], x_raw[n][:, :, :cut])
             interleave(nc.scalar.copy, grouped[:, cut:], x_raw[n][:, :, cut:])
@@ -133,16 +143,15 @@ def tile_picked_gcn_mlp_gelu_sub_l_kernel(
                 in_=x_g[n][:].rearrange("p t j -> p (t j)"),
             )
 
-        copy_x(0)
-        quantize_chunk(0)
-        for n in range(1, len(x_pieces)):
+        for n in range(len(x_pieces)):
             copy_x(n)
-            quantize_x(n - 1)
-        quantize_x(len(x_pieces) - 1)
+            if n == W0Q:
+                quantize_chunk(0)
+            quantize_x(n)
 
         def project(i, parts=1):
             acc = ps_h.tile([P, T], F32, name="acc_h")
-            h = stage.tile([P, T], F32, name="h")
+            h = hpool.tile([P, T], F32, name="h")
             width = T // parts
             for part in range(parts):
                 nodes = slice(part * width, (part + 1) * width)
@@ -205,42 +214,43 @@ def tile_picked_gcn_mlp_gelu_sub_l_kernel(
                 in_=grouped[:].rearrange("p v t -> p (v t)"),
             )
 
-        h_next = project(0, parts=2)
-        for dst, src in copy_chunk(1):
-            interleave(nc.scalar.copy, dst, src)
+        hs = {0: project(0, parts=2)}
         n_tiles = H // P
         w2_g = held.tile([P, Q, N, PACK], BF16, align_bytes=64)
         w2_codes = held.tile([P, Q, N], U32, align_bytes=64)
         w2_scales = held.tile([P, Q, N], U8, align_bytes=64)
-        background = copy_chunk(2) + copy_chunk(3) + [(w2_g[:, q], w2_raw[:, q]) for q in range(Q)]
         pending = None
+        copied = []
         for i in range(n_tiles):
-            h = h_next
             prods = []
             for d in range(D):
-                if (i, d) == (0, 4):
-                    quantize_chunk(1)
-                if (i, d) == (1, 4):
-                    quantize_chunk(2)
-                if (i, d) == (1, 5):
-                    background += copy_chunk(4)
-                if (i, d) == (3, 1):
-                    quantize_chunk(3)
-                if (i, d) == (5, 1):
-                    quantize_chunk(4)
-                if (i, d) == (5, 3):
+                slot = i * D + d
+                if slot in QUANT_SLOTS:
+                    n = QUANT_SLOTS.index(slot) + 1
+                    quantize_chunk(n)
+                if slot in PROJECT_SLOTS:
+                    n = PROJECT_SLOTS.index(slot) + 1
+                    hs[n] = project(n)
+                if slot == Z_SLOT:
                     quantize_z(0, pending)
-                if (i, d) == (6, 0):
+                if slot == W2_SLOT:
                     nc.vector.quantize_mx(
                         out=w2_codes[:].rearrange("p q m -> p (q m)").bitcast(FP8X4),
                         scales=w2_scales[:].rearrange("p q m -> p (q m)"),
                         in_=w2_g[:].rearrange("p q m j -> p (q m j)"),
                     )
-                prods.append(gather(h, d))
-                if d == 4 and i + 1 < n_tiles:
-                    h_next = project(i + 1)
-                if i * D + d >= 2 and d % 2 == 0 and background:
-                    interleave(nc.scalar.copy, *background.pop(0))
+                prods.append(gather(hs[i], d))
+                for k in range(COPY_SLOTS.count(slot)):
+                    n = len(copied)
+                    if n < C * (len(CHUNKS) - 1):
+                        if n % C == 0:
+                            tasks = copy_chunk(n // C + 1)
+                        task = tasks[n % C]
+                    else:
+                        m = n - C * (len(CHUNKS) - 1)
+                        task = (w2_g[:, m], w2_raw[:, m])
+                    interleave(nc.scalar.copy, *task)
+                    copied.append(n)
             add_up(i, prods)
             if i % PACK == PACK - 1:
                 pending = turn_back(i // PACK)

@@ -10,6 +10,8 @@ U8 = mybir.dt.uint8
 U16 = mybir.dt.uint16
 FP8X4 = mybir.dt.float8_e4m3fn_x4
 MULT = mybir.AluOpType.mult
+ADD = mybir.AluOpType.add
+COPY = mybir.ActivationFunctionType.Copy
 GELU = mybir.ActivationFunctionType.Gelu_apprx_tanh
 
 FLOPS = 2 * K * H * T + 2 * D * H * V + 2 * H * N * V
@@ -20,16 +22,15 @@ PASS = P * PACK
 C = K // PASS
 Q = H // PASS
 HALF = V // 2
-CHUNKS = (256, 256, 256, 256)
-COPY_SLOTS = (1, 2, 4, 6, 8, 9, 11, 13, 15, 16, 18, 20, 24, 27)
-QUANT_SLOTS = (8, 18, 28)
-PROJECT_SLOTS = (2, 10, 14, 20, 26, 30, 38)
+TOKEN_SLOTS = (0, 7, 9, 12, 17, 19)
+QUANT_SLOTS = (6, 9)
+BIG_SLOTS = (12, 16, 19, 21)
+PROJECT_SLOTS = (0, 9, 10, 21, 29, 30, 34)
+Z_SLOT = 30
+W2_SLOT = 43
 X_CUT = 11
-Z_SLOT = 33
-W2_SLOT = 40
-W0Q = 0
-GATE_CUT = 6
-PIECES = (512, 512, 512, 256, 256)
+CHUNKS = (256, 256)
+XP = (512, 512, 512, 256, 256)
 
 
 def tile_picked_gcn_mlp_gelu_sub_l_kernel(
@@ -39,9 +40,8 @@ def tile_picked_gcn_mlp_gelu_sub_l_kernel(
     lists_dram = (pos1, pos2, pos3, pos4, pos5, pos6)
     with (
         tc.tile_pool(name="held", bufs=1) as held,
-        tc.tile_pool(name="wraw", bufs=3) as wraw,
+        tc.tile_pool(name="four", bufs=4) as four,
         tc.tile_pool(name="stage", bufs=2) as stage,
-        tc.tile_pool(name="hpool", bufs=4) as hpool,
         tc.psum_pool(name="ps_h", bufs=2) as ps_h,
         tc.psum_pool(name="ps_z", bufs=1) as ps_z,
     ):
@@ -52,26 +52,25 @@ def tile_picked_gcn_mlp_gelu_sub_l_kernel(
         ident = held.tile([P, P], F32)
         make_identity(nc, ident[:])
 
-        starts = [sum(CHUNKS[:n]) for n in range(len(CHUNKS))]
-        w_raw = {}
+        w_raw = []
 
-        def load_chunk(n):
-            raw = wraw.tile([P, C, PACK, CHUNKS[n]], F32, name=f"w_raw{CHUNKS[n]}")
+        def load_block(i):
+            width = CHUNKS[i]
+            w0 = sum(CHUNKS[:i])
+            raw = stage.tile([P, C, PACK, width], F32, name=f"w_raw{width}")
             for c in range(C):
                 nc.sync.dma_start(
                     out=raw[:, c],
-                    in_=w1[c * PASS : (c + 1) * PASS, starts[n] : starts[n] + CHUNKS[n]].rearrange(
-                        "(p j) w -> p j w", j=PACK
-                    ),
+                    in_=w1[c * PASS : (c + 1) * PASS, w0 : w0 + width].rearrange("(p j) w -> p j w", j=PACK),
                 )
-            w_raw[n] = raw
+            w_raw.append(raw)
 
-        load_chunk(0)
-        x_pieces = [(sum(PIECES[:n]) // T, sum(PIECES[:n]) % T, PIECES[n]) for n in range(len(PIECES))]
+        load_block(0)
+        x_pieces = [(sum(XP[:n]) // T, sum(XP[:n]) % T, XP[n]) for n in range(len(XP))]
         x_raw = []
         lists = []
         for n, (c, t0, width) in enumerate(x_pieces):
-            raw = held.tile([P, PACK, width], F32, name=f"x_raw{n}")
+            raw = four.tile([P, PACK, width], F32, name="raw" if width == T else f"x_raw{n}")
             nc.sync.dma_start(
                 out=raw[:],
                 in_=xT[c * PASS : (c + 1) * PASS, t0 : t0 + width].rearrange("(p j) t -> p j t", j=PACK),
@@ -83,14 +82,19 @@ def tile_picked_gcn_mlp_gelu_sub_l_kernel(
                     nc.sync.dma_start(lst[:], lists_dram[d])
                     lists.append(lst)
         gates = held.tile([P, D, V], F32)
-        nc.sync.dma_start(out=gates[:, :GATE_CUT], in_=gate[:GATE_CUT].rearrange("d p v -> p d v"))
-        for n in range(1, len(CHUNKS)):
-            load_chunk(n)
-            if n == 1 and GATE_CUT < D:
-                nc.sync.dma_start(out=gates[:, GATE_CUT:], in_=gate[GATE_CUT:].rearrange("d p v -> p d v"))
-            if n == len(CHUNKS) - 2:
-                w2_raw = held.tile([P, Q, PACK, N], F32)
-                nc.sync.dma_start(out=w2_raw[:], in_=w2.rearrange("(q p j) m -> p q j m", q=Q, j=PACK))
+        nc.sync.dma_start(out=gates[:], in_=gate.rearrange("d p v -> p d v"))
+        load_block(1)
+        for n in range(2, len(CHUNKS)):
+            load_block(n)
+        big_raw = []
+        for c in range(C):
+            raw = four.tile([P, PACK, PASS], F32, name="raw")
+            nc.sync.dma_start(
+                out=raw[:], in_=w1[c * PASS : (c + 1) * PASS, PASS:].rearrange("(p j) w -> p j w", j=PACK)
+            )
+            big_raw.append(raw)
+        w2_raw = held.tile([P, Q, PACK, N], F32)
+        nc.sync.dma_start(out=w2_raw[:], in_=w2.rearrange("(q p j) m -> p q j m", q=Q, j=PACK))
 
         def interleave(copy, dst, src):
             copy(
@@ -99,67 +103,81 @@ def tile_picked_gcn_mlp_gelu_sub_l_kernel(
             )
 
         w_codes, w_scales = [], []
+        for i in range(len(CHUNKS)):
+            codes = held.tile([P, C, CHUNKS[i]], U32, name=f"w_codes{i}", align_bytes=64)
+            scales = held.tile([P, C, CHUNKS[i]], U8, name=f"w_scales{i}", align_bytes=64)
+            w_codes.append(codes)
+            w_scales.append(scales)
+        groups = {}
 
-        w_g = {}
+        def copy_w(copy, i, c):
+            if c == 0:
+                groups[i] = held.tile([P, C, 256, PACK], BF16, name=f"group_w{i}", align_bytes=64)
+            interleave(copy, groups[i][:, c], w_raw[i][:, c])
 
-        def copy_chunk(n):
-            width = CHUNKS[n]
-            grouped = stage.tile([P, C, width, PACK], BF16, name=f"w_g{width}", align_bytes=64)
-            w_g[n] = grouped
-            return [(grouped[:, c], w_raw[n][:, c]) for c in range(C)]
-
-        def quantize_chunk(n):
-            width = CHUNKS[n]
-            codes = held.tile([P, C, width], U32, name=f"w_codes{n}", align_bytes=64)
-            scales = held.tile([P, C, width], U8, name=f"w_scales{n}", align_bytes=64)
+        def quantize_w(i, s):
             nc.vector.quantize_mx(
-                out=codes[:].rearrange("p c w -> p (c w)").bitcast(FP8X4),
-                scales=scales[:].rearrange("p c w -> p (c w)"),
-                in_=w_g[n][:].rearrange("p c w j -> p (c w j)"),
+                out=w_codes[i][:, 2 * s : 2 * s + 2].rearrange("p c w -> p (c w)").bitcast(FP8X4),
+                scales=w_scales[i][:, 2 * s : 2 * s + 2].rearrange("p c w -> p (c w)"),
+                in_=groups[i][:, 2 * s : 2 * s + 2].rearrange("p c w j -> p (c w j)"),
             )
-            for b in range(width // P):
-                w_codes.append(codes[:, :, b * P : (b + 1) * P])
-                w_scales.append(scales[:, :, b * P : (b + 1) * P])
 
-        for dst, src in copy_chunk(0):
-            interleave(nc.scalar.copy, dst, src)
+        for c in range(C):
+            copy_w(nc.scalar.copy, 0, c)
+        for s in range(2):
+            quantize_w(0, s)
         x_codes = held.tile([P, C, T], U32, align_bytes=64)
         x_scales = held.tile([P, C, T], U8, align_bytes=64)
-        x_g = []
-
-        def copy_x(n):
-            width = x_pieces[n][2]
+        for n, (c, t0, width) in enumerate(x_pieces):
             cut = width * X_CUT // 16
             grouped = held.tile([P, width, PACK], BF16, name=f"x_g{n}", align_bytes=64)
             interleave(nc.vector.tensor_copy, grouped[:, :cut], x_raw[n][:, :, :cut])
             interleave(nc.scalar.copy, grouped[:, cut:], x_raw[n][:, :, cut:])
-            x_g.append(grouped)
-
-        def quantize_x(n):
-            c, t0, width = x_pieces[n]
             nc.vector.quantize_mx(
                 out=x_codes[:, c, t0 : t0 + width].bitcast(FP8X4),
                 scales=x_scales[:, c, t0 : t0 + width],
-                in_=x_g[n][:].rearrange("p t j -> p (t j)"),
+                in_=grouped[:].rearrange("p t j -> p (t j)"),
             )
 
-        for n in range(len(x_pieces)):
-            copy_x(n)
-            if n == W0Q:
-                quantize_chunk(0)
-            quantize_x(n)
+        big_codes = held.tile([P, C, PASS], U32, align_bytes=64)
+        big_scales = held.tile([P, C, PASS], U8, align_bytes=64)
+
+        def copy_big(copy, c, part):
+            if part == 0:
+                groups["big", c] = held.tile([P, PACK, P, PACK], BF16, name=f"group_big{c}", align_bytes=64)
+            m = slice(part * 64, (part + 1) * 64)
+            w = slice(part * 256, (part + 1) * 256)
+            copy(
+                out=groups["big", c][:, :, m].rearrange("p t m j -> p m j t"),
+                in_=big_raw[c][:, :, w].rearrange("p j (m t) -> p m j t", t=PACK),
+            )
+
+        def quantize_big(c):
+            nc.vector.quantize_mx(
+                out=big_codes[:, c].bitcast(FP8X4),
+                scales=big_scales[:, c],
+                in_=groups["big", c][:].rearrange("p t m j -> p (t m j)"),
+            )
 
         def project(i, parts=1):
             acc = ps_h.tile([P, T], F32, name="acc_h")
-            h = hpool.tile([P, T], F32, name="h")
+            h = four.tile([P, T], F32, name="h")
+            if i < PACK:
+                cols = slice(i % 2 * P, (i % 2 + 1) * P)
+                codes = [w_codes[i // 2][:, c, cols] for c in range(C)]
+                scales = [w_scales[i // 2][:, c, cols] for c in range(C)]
+            else:
+                cols = slice((i - PACK) * P, (i - PACK + 1) * P)
+                codes = [big_codes[:, c, cols] for c in range(C)]
+                scales = [big_scales[:, c, cols] for c in range(C)]
             width = T // parts
             for part in range(parts):
                 nodes = slice(part * width, (part + 1) * width)
                 for c in range(C):
                     nc.tensor.matmul_mx(
                         out=acc[:, nodes],
-                        lhsT=w_codes[i][:, c].bitcast(FP8X4),
-                        lhsT_scale=w_scales[i][:, c],
+                        lhsT=codes[c].bitcast(FP8X4),
+                        lhsT_scale=scales[c],
                         rhs=x_codes[:, c, nodes].bitcast(FP8X4),
                         rhs_scale=x_scales[:, c, nodes],
                         start=(c == 0),
@@ -171,90 +189,131 @@ def tile_picked_gcn_mlp_gelu_sub_l_kernel(
         zT = [held.tile([P, Q, PACK, P], F32, name=f"zT{half}") for half in range(2)]
         z_codes = held.tile([P, Q, V], U32, align_bytes=64)
         z_scales = held.tile([P, Q, V], U8, align_bytes=64)
+        z_g = [held.tile([P, V, PACK], BF16, name=f"z_g{q}", align_bytes=64) for q in range(Q)]
 
-        def gather(h, d):
-            prod = stage.tile([P, V], F32, name=f"prod{d}")
-            nc.vector.tensor_tensor(prod[:], h[:].indirect(lists[d][:]), gates[:, d], MULT)
-            return prod
+        def gather(out, h, d):
+            nc.vector.tensor_tensor(out, h[:].indirect(lists[d][:]), gates[:, d], MULT)
 
         def add_up(i, prods):
-            q, b = divmod(i, PACK)
-            accs = [ps_z.tile([P, P], F32, name=f"acc_z{half}") for half in range(2)]
-            for d in range(D):
+            for half in range(2):
+                accs[half] = ps_z.tile([P, P], F32, name=f"acc_z{half}")
+            for d, prod in enumerate(prods):
                 for half in range(2):
                     nc.tensor.matmul(
                         accs[half][:],
-                        lhsT=prods[d][:, half * HALF : (half + 1) * HALF],
+                        lhsT=prod[:, half * HALF : (half + 1) * HALF],
                         rhs=ident[:],
                         start=(d == 0),
-                        stop=(d == D - 1),
+                        stop=(d == len(prods) - 1),
                         is_transpose=True,
                     )
             for half in range(2):
-                copy = nc.vector.tensor_copy if (half and i == H // P - 1) else nc.scalar.copy
+                keep_sum(nc.scalar.copy, i, half, accs[half])
+
+        def keep_sum(copy, i, half, acc):
+            q, b = divmod(i, PACK)
+            if q == 0:
                 copy(
-                    out=zT[half][:, q, :, 32 * b : 32 * (b + 1)],
-                    in_=accs[half][:].rearrange("p (m t) -> p t m", t=PACK),
+                    out=zT[half][:, 0, :, 32 * b : 32 * (b + 1)],
+                    in_=acc[:].rearrange("p (m t) -> p t m", t=PACK),
                 )
+            else:
+                copy(out=zT[half][:, 1, b], in_=acc[:])
 
-        def turn_back(q):
-            grouped = stage.tile([P, V, PACK], BF16, name="z_g", align_bytes=64)
-            for half in range(2):
-                back = ps_z.tile([P, PACK, HALF], F32, name=f"back{half}")
-                for t in range(PACK):
-                    nc.tensor.transpose(back[:, t], zT[half][:, q, t], ident[:])
-                copy = nc.vector.tensor_copy if (half and q) else nc.scalar.copy
-                copy(out=grouped[:, half * HALF : (half + 1) * HALF], in_=back[:].rearrange("p t v -> p v t"))
-            return grouped
+        def interleave_z(copy, q, half, back, planes):
+            v = slice(half * HALF, (half + 1) * HALF)
+            copy(out=z_g[q][:, v, planes], in_=back[:, planes].rearrange("p t v -> p v t"))
 
-        def quantize_z(q, grouped):
+        accs = [None, None]
+        backs = [None, None]
+
+        def quantize_z(q, v0=0, width=V):
             nc.vector.quantize_mx(
-                out=z_codes[:, q].bitcast(FP8X4),
-                scales=z_scales[:, q],
-                in_=grouped[:].rearrange("p v t -> p (v t)"),
+                out=z_codes[:, q, v0 : v0 + width].bitcast(FP8X4),
+                scales=z_scales[:, q, v0 : v0 + width],
+                in_=z_g[q][:, v0 : v0 + width].rearrange("p v t -> p (v t)"),
             )
 
         hs = {0: project(0, parts=2)}
         n_tiles = H // P
-        w2_g = held.tile([P, Q, N, PACK], BF16, align_bytes=64)
         w2_codes = held.tile([P, Q, N], U32, align_bytes=64)
         w2_scales = held.tile([P, Q, N], U8, align_bytes=64)
-        pending = None
-        copied = []
-        for i in range(n_tiles):
-            prods = []
-            for d in range(D):
-                slot = i * D + d
+        late = held.tile([P, 2, V], F32)
+        prods = []
+        seq = [(i, d) for i in range(n_tiles) for d in range(D) if not (i >= 6 and d == D - 1)] + [(6, D - 1), (7, D - 1)]
+        for slot in range(48):
+                i, d = seq[slot]
                 if slot in QUANT_SLOTS:
-                    n = QUANT_SLOTS.index(slot) + 1
-                    quantize_chunk(n)
+                    quantize_w(1, QUANT_SLOTS.index(slot))
+                for c in range(C):
+                    if slot == BIG_SLOTS[c]:
+                        quantize_big(c)
                 if slot in PROJECT_SLOTS:
                     n = PROJECT_SLOTS.index(slot) + 1
                     hs[n] = project(n)
                 if slot == Z_SLOT:
-                    quantize_z(0, pending)
+                    quantize_z(0)
                 if slot == W2_SLOT:
                     nc.vector.quantize_mx(
                         out=w2_codes[:].rearrange("p q m -> p (q m)").bitcast(FP8X4),
                         scales=w2_scales[:].rearrange("p q m -> p (q m)"),
-                        in_=w2_g[:].rearrange("p q m j -> p (q m j)"),
+                        in_=groups["w2"][:].rearrange("p q m j -> p (q m j)"),
                     )
-                prods.append(gather(hs[i], d))
-                for k in range(COPY_SLOTS.count(slot)):
-                    n = len(copied)
-                    if n < C * (len(CHUNKS) - 1):
-                        if n % C == 0:
-                            tasks = copy_chunk(n // C + 1)
-                        task = tasks[n % C]
+                if slot >= 46:
+                    gather(late[:, i - 6], hs[i], d)
+                else:
+                    if slot == QUANT_SLOTS[1]:
+                        prod = held.tile([P, V], F32, name="group_w1", align_bytes=64)
+                    elif slot == BIG_SLOTS[3]:
+                        prod = held.tile([P, V], F32, name="group_big3", align_bytes=64)
                     else:
-                        m = n - C * (len(CHUNKS) - 1)
-                        task = (w2_g[:, m], w2_raw[:, m])
-                    interleave(nc.scalar.copy, *task)
-                    copied.append(n)
-            add_up(i, prods)
-            if i % PACK == PACK - 1:
-                pending = turn_back(i // PACK)
-        quantize_z(1, pending)
+                        prod = stage.tile([P, V], F32, name=f"prod{d}")
+                    gather(prod[:], hs[i], d)
+                    prods.append(prod)
+                if slot in TOKEN_SLOTS:
+                    token = stage.tile([P, 1], F32, name="token")
+                    nc.gpsimd.tensor_scalar(token[:], prod[:, :1], 0.0, 1.0, MULT, ADD)
+
+                    def copy(out, in_):
+                        nc.scalar.activation(out, in_, COPY, scale=token[:])
+
+                    n = TOKEN_SLOTS.index(slot)
+                    if n == 0:
+                        for c in range(C):
+                            copy_w(copy, 1, c)
+                    elif n < 5:
+                        for part in range(2):
+                            copy_big(copy, n - 1, part)
+                    else:
+                        groups["w2"] = stage.tile([P, Q, N, PACK], BF16, name="grouped", align_bytes=64)
+                        for q in range(Q):
+                            interleave(copy, groups["w2"][:, q], w2_raw[:, q])
+                if (i < 6 and d == D - 1) or (i >= 6 and d == D - 2):
+                    add_up(i, prods)
+                    prods = []
+                    if i % PACK == 0:
+                        for half in range(2):
+                            backs[half] = ps_z.tile([P, PACK, HALF], F32, name=f"back{half}")
+                    if i == PACK - 1:
+                        for half in range(2):
+                            for t in range(PACK):
+                                nc.tensor.transpose(backs[half][:, t], zT[half][:, 0, t], ident[:])
+                            interleave_z(nc.scalar.copy, 0, half, backs[half], slice(0, PACK))
+                    if i >= PACK:
+                        for half in range(2):
+                            nc.tensor.transpose(backs[half][:, i - PACK], zT[half][:, 1, i - PACK], ident[:])
+                    if i == 5:
+                        for half in range(2):
+                            interleave_z(nc.scalar.copy, 1, half, backs[half], slice(0, 2))
+        for half in range(2):
+            v = slice(half * HALF, (half + 1) * HALF)
+            nc.vector.tensor_tensor(
+                z_g[1][:, v, 2:4],
+                backs[half][:, 2:4].rearrange("p t v -> p v t"),
+                late[:, :, v].rearrange("p t v -> p v t"),
+                ADD,
+            )
+        quantize_z(1)
         for b in range(N // P):
             acc = ps_z.tile([P, V], F32, name=f"acc_o{b}")
             for q in range(Q):

@@ -272,7 +272,7 @@ def tile_picked_gcn_mlp_gelu_sub_l_kernel(
                     prods.append(prod)
                 if slot in TOKEN_SLOTS:
                     token = stage.tile([P, 1], F32, name="token")
-                    nc.gpsimd.tensor_scalar(token[:], prod[:, :1], 0.0, 1.0, MULT, ADD)
+                    nc.scalar.activation(token[:], prod[:, :1], COPY, bias=1.0, scale=0.0)
 
                     def copy(out, in_):
                         nc.scalar.activation(out, in_, COPY, scale=token[:])

@@ -6,12 +6,11 @@ K, T, D, V, H, N = 2048, 512, 6, 256, 1024, 256
 F32 = mybir.dt.float32
 BF16 = mybir.dt.bfloat16
 U32 = mybir.dt.uint32
-U8 = mybir.dt.uint8
 U16 = mybir.dt.uint16
+U8 = mybir.dt.uint8
 FP8X4 = mybir.dt.float8_e4m3fn_x4
 MULT = mybir.AluOpType.mult
 ADD = mybir.AluOpType.add
-COPY = mybir.ActivationFunctionType.Copy
 GELU = mybir.ActivationFunctionType.Gelu_apprx_tanh
 
 FLOPS = 2 * K * H * T + 2 * D * H * V + 2 * H * N * V
@@ -19,316 +18,298 @@ FLOPS = 2 * K * H * T + 2 * D * H * V + 2 * H * N * V
 P = 128
 PACK = 4
 PASS = P * PACK
-C = K // PASS
-Q = H // PASS
+K_PASSES = K // PASS
+I_PASSES = H // PASS
+BLOCKS = H // P
+CHUNK = 256
 HALF = V // 2
-TOKEN_SLOTS = (0, 7, 9, 12, 17, 19)
-QUANT_SLOTS = (6, 9)
-BIG_SLOTS = (12, 16, 19, 21)
-PROJECT_SLOTS = (0, 9, 10, 21, 29, 30, 34)
-Z_SLOT = 30
-W2_SLOT = 43
-X_CUT = 11
-CHUNKS = (256, 256)
-XP = (512, 512, 512, 256, 256)
+
+X_PIECES = ((0, 0, T), (1, 0, T), (2, 0, T), (3, 0, T // 2), (3, T // 2, T // 2))
+VECTOR_SHARE = 11
+
+GATHERS = [(b, d) for b in range(BLOCKS) for d in range(D) if b < BLOCKS - 2 or d < D - 1] + [
+    (b, D - 1) for b in (BLOCKS - 2, BLOCKS - 1)
+]
+LATE = len(GATHERS) - 2
 
 
 def tile_picked_gcn_mlp_gelu_sub_l_kernel(
     tc, xT, w1, w2, gate, pos1, pos2, pos3, pos4, pos5, pos6, out
 ):
     nc = tc.nc
-    lists_dram = (pos1, pos2, pos3, pos4, pos5, pos6)
     with (
         tc.tile_pool(name="held", bufs=1) as held,
         tc.tile_pool(name="four", bufs=4) as four,
-        tc.tile_pool(name="stage", bufs=2) as stage,
-        tc.psum_pool(name="ps_h", bufs=2) as ps_h,
-        tc.psum_pool(name="ps_z", bufs=1) as ps_z,
+        tc.tile_pool(name="two", bufs=2) as two,
+        tc.psum_pool(name="psum_h", bufs=2) as psum_h,
+        tc.psum_pool(name="psum_z", bufs=1) as psum_z,
     ):
-        warm_in = held.tile([P, 1], F32)
-        warm_out = held.tile([P, 1], F32)
-        nc.vector.memset(warm_in[:], 0.0)
-        nc.scalar.activation(warm_out[:], warm_in[:], GELU)
-        ident = held.tile([P, P], F32)
-        make_identity(nc, ident[:])
+        zero = held.tile([P, 1], F32)
+        unused = held.tile([P, 1], F32)
+        nc.vector.memset(zero[:], 0.0)
+        nc.scalar.activation(unused[:], zero[:], GELU)
+        identity = held.tile([P, P], F32)
+        make_identity(nc, identity[:])
 
-        w_raw = []
+        def rows_of_pass(matrix, c, columns):
+            return matrix[c * PASS : (c + 1) * PASS, columns].rearrange("(p j) w -> p j w", j=PACK)
 
-        def load_block(i):
-            width = CHUNKS[i]
-            w0 = sum(CHUNKS[:i])
-            raw = stage.tile([P, C, PACK, width], F32, name=f"w_raw{width}")
-            for c in range(C):
-                nc.sync.dma_start(
-                    out=raw[:, c],
-                    in_=w1[c * PASS : (c + 1) * PASS, w0 : w0 + width].rearrange("(p j) w -> p j w", j=PACK),
-                )
-            w_raw.append(raw)
+        lower_raw = []
 
-        load_block(0)
-        x_pieces = [(sum(XP[:n]) // T, sum(XP[:n]) % T, XP[n]) for n in range(len(XP))]
+        def load_lower(n):
+            raw = two.tile([P, K_PASSES, PACK, CHUNK], F32, name="lower_raw")
+            for c in range(K_PASSES):
+                nc.sync.dma_start(out=raw[:, c], in_=rows_of_pass(w1, c, slice(n * CHUNK, (n + 1) * CHUNK)))
+            lower_raw.append(raw)
+
+        load_lower(0)
         x_raw = []
         lists = []
-        for n, (c, t0, width) in enumerate(x_pieces):
-            raw = four.tile([P, PACK, width], F32, name="raw" if width == T else f"x_raw{n}")
-            nc.sync.dma_start(
-                out=raw[:],
-                in_=xT[c * PASS : (c + 1) * PASS, t0 : t0 + width].rearrange("(p j) t -> p j t", j=PACK),
-            )
+        for n, (c, t0, nodes) in enumerate(X_PIECES):
+            raw = four.tile([P, PACK, nodes], F32, name="raw" if nodes == T else f"x_raw{t0}")
+            nc.sync.dma_start(out=raw[:], in_=rows_of_pass(xT, c, slice(t0, t0 + nodes)))
             x_raw.append(raw)
             if n == 1:
-                for d in range(D):
-                    lst = held.tile([P, V // 16], U16, name=f"list{d}")
-                    nc.sync.dma_start(lst[:], lists_dram[d])
-                    lists.append(lst)
+                for d, pos in enumerate((pos1, pos2, pos3, pos4, pos5, pos6)):
+                    offsets = held.tile([P, V // 16], U16, name=f"offsets{d}")
+                    nc.sync.dma_start(offsets[:], pos)
+                    lists.append(offsets)
         gates = held.tile([P, D, V], F32)
         nc.sync.dma_start(out=gates[:], in_=gate.rearrange("d p v -> p d v"))
-        load_block(1)
-        for n in range(2, len(CHUNKS)):
-            load_block(n)
-        big_raw = []
-        for c in range(C):
+        load_lower(1)
+        upper_raw = []
+        for c in range(K_PASSES):
             raw = four.tile([P, PACK, PASS], F32, name="raw")
-            nc.sync.dma_start(
-                out=raw[:], in_=w1[c * PASS : (c + 1) * PASS, PASS:].rearrange("(p j) w -> p j w", j=PACK)
-            )
-            big_raw.append(raw)
-        w2_raw = held.tile([P, Q, PACK, N], F32)
-        nc.sync.dma_start(out=w2_raw[:], in_=w2.rearrange("(q p j) m -> p q j m", q=Q, j=PACK))
+            nc.sync.dma_start(out=raw[:], in_=rows_of_pass(w1, c, slice(PASS, H)))
+            upper_raw.append(raw)
+        w2_raw = held.tile([P, I_PASSES, PACK, N], F32)
+        nc.sync.dma_start(out=w2_raw[:], in_=w2.rearrange("(q p j) m -> p q j m", q=I_PASSES, j=PACK))
 
-        def interleave(copy, dst, src):
+        def interleave(copy, grouped, raw):
             copy(
-                out=dst.rearrange("p (c i) j -> p c j i", i=4),
-                in_=src.rearrange("p j (c i) -> p c j i", i=4),
+                out=grouped.rearrange("p (c i) j -> p c j i", i=4),
+                in_=raw.rearrange("p j (c i) -> p c j i", i=4),
             )
 
-        w_codes, w_scales = [], []
-        for i in range(len(CHUNKS)):
-            codes = held.tile([P, C, CHUNKS[i]], U32, name=f"w_codes{i}", align_bytes=64)
-            scales = held.tile([P, C, CHUNKS[i]], U8, name=f"w_scales{i}", align_bytes=64)
-            w_codes.append(codes)
-            w_scales.append(scales)
-        groups = {}
+        def quantize(codes, scales, grouped):
+            nc.vector.quantize_mx(out=codes.bitcast(FP8X4), scales=scales, in_=grouped)
 
-        def copy_w(copy, i, c):
-            if c == 0:
-                groups[i] = held.tile([P, C, 256, PACK], BF16, name=f"group_w{i}", align_bytes=64)
-            interleave(copy, groups[i][:, c], w_raw[i][:, c])
+        lower_codes = [held.tile([P, K_PASSES, CHUNK], U32, name=f"lower_codes{n}", align_bytes=64) for n in range(2)]
+        lower_scales = [held.tile([P, K_PASSES, CHUNK], U8, name=f"lower_scales{n}", align_bytes=64) for n in range(2)]
+        lower_grouped = {}
 
-        def quantize_w(i, s):
-            nc.vector.quantize_mx(
-                out=w_codes[i][:, 2 * s : 2 * s + 2].rearrange("p c w -> p (c w)").bitcast(FP8X4),
-                scales=w_scales[i][:, 2 * s : 2 * s + 2].rearrange("p c w -> p (c w)"),
-                in_=groups[i][:, 2 * s : 2 * s + 2].rearrange("p c w j -> p (c w j)"),
+        def copy_lower(n):
+            lower_grouped[n] = held.tile([P, K_PASSES, CHUNK, PACK], BF16, name=f"lower_grouped{n}", align_bytes=64)
+            for c in range(K_PASSES):
+                interleave(nc.scalar.copy, lower_grouped[n][:, c], lower_raw[n][:, c])
+
+        def quantize_lower(n, s):
+            passes = slice(2 * s, 2 * s + 2)
+            quantize(
+                lower_codes[n][:, passes].rearrange("p c w -> p (c w)"),
+                lower_scales[n][:, passes].rearrange("p c w -> p (c w)"),
+                lower_grouped[n][:, passes].rearrange("p c w j -> p (c w j)"),
             )
 
-        for c in range(C):
-            copy_w(nc.scalar.copy, 0, c)
+        upper_codes = held.tile([P, K_PASSES, PASS], U32, align_bytes=64)
+        upper_scales = held.tile([P, K_PASSES, PASS], U8, align_bytes=64)
+        upper_grouped = {}
+
+        def copy_upper(c):
+            upper_grouped[c] = held.tile([P, PACK, P, PACK], BF16, name=f"upper_grouped{c}", align_bytes=64)
+            for half in range(2):
+                m = slice(half * P // 2, (half + 1) * P // 2)
+                columns = slice(half * PASS // 2, (half + 1) * PASS // 2)
+                nc.scalar.copy(
+                    out=upper_grouped[c][:, :, m].rearrange("p t m j -> p m j t"),
+                    in_=upper_raw[c][:, :, columns].rearrange("p j (m t) -> p m j t", t=PACK),
+                )
+
+        def quantize_upper(c):
+            quantize(upper_codes[:, c], upper_scales[:, c], upper_grouped[c][:].rearrange("p t m j -> p (t m j)"))
+
+        w2_codes = held.tile([P, I_PASSES, N], U32, align_bytes=64)
+        w2_scales = held.tile([P, I_PASSES, N], U8, align_bytes=64)
+        w2_grouped = held.tile([P, I_PASSES, N, PACK], BF16, align_bytes=64)
+
+        def copy_w2():
+            for q in range(I_PASSES):
+                interleave(nc.scalar.copy, w2_grouped[:, q], w2_raw[:, q])
+
+        def quantize_w2():
+            quantize(
+                w2_codes[:].rearrange("p q m -> p (q m)"),
+                w2_scales[:].rearrange("p q m -> p (q m)"),
+                w2_grouped[:].rearrange("p q m j -> p (q m j)"),
+            )
+
+        copy_lower(0)
         for s in range(2):
-            quantize_w(0, s)
-        x_codes = held.tile([P, C, T], U32, align_bytes=64)
-        x_scales = held.tile([P, C, T], U8, align_bytes=64)
-        for n, (c, t0, width) in enumerate(x_pieces):
-            cut = width * X_CUT // 16
-            grouped = held.tile([P, width, PACK], BF16, name=f"x_g{n}", align_bytes=64)
-            interleave(nc.vector.tensor_copy, grouped[:, :cut], x_raw[n][:, :, :cut])
-            interleave(nc.scalar.copy, grouped[:, cut:], x_raw[n][:, :, cut:])
-            nc.vector.quantize_mx(
-                out=x_codes[:, c, t0 : t0 + width].bitcast(FP8X4),
-                scales=x_scales[:, c, t0 : t0 + width],
-                in_=grouped[:].rearrange("p t j -> p (t j)"),
+            quantize_lower(0, s)
+        x_codes = held.tile([P, K_PASSES, T], U32, align_bytes=64)
+        x_scales = held.tile([P, K_PASSES, T], U8, align_bytes=64)
+        for n, (c, t0, nodes) in enumerate(X_PIECES):
+            cut = nodes * VECTOR_SHARE // 16
+            x_grouped = held.tile([P, nodes, PACK], BF16, name=f"x_grouped{n}", align_bytes=64)
+            interleave(nc.vector.tensor_copy, x_grouped[:, :cut], x_raw[n][:, :, :cut])
+            interleave(nc.scalar.copy, x_grouped[:, cut:], x_raw[n][:, :, cut:])
+            quantize(
+                x_codes[:, c, t0 : t0 + nodes],
+                x_scales[:, c, t0 : t0 + nodes],
+                x_grouped[:].rearrange("p t j -> p (t j)"),
             )
 
-        big_codes = held.tile([P, C, PASS], U32, align_bytes=64)
-        big_scales = held.tile([P, C, PASS], U8, align_bytes=64)
+        h = {}
 
-        def copy_big(copy, c, part):
-            if part == 0:
-                groups["big", c] = held.tile([P, PACK, P, PACK], BF16, name=f"group_big{c}", align_bytes=64)
-            m = slice(part * 64, (part + 1) * 64)
-            w = slice(part * 256, (part + 1) * 256)
-            copy(
-                out=groups["big", c][:, :, m].rearrange("p t m j -> p m j t"),
-                in_=big_raw[c][:, :, w].rearrange("p j (m t) -> p m j t", t=PACK),
-            )
-
-        def quantize_big(c):
-            nc.vector.quantize_mx(
-                out=big_codes[:, c].bitcast(FP8X4),
-                scales=big_scales[:, c],
-                in_=groups["big", c][:].rearrange("p t m j -> p (t m j)"),
-            )
-
-        def project(i, parts=1):
-            acc = ps_h.tile([P, T], F32, name="acc_h")
-            h = four.tile([P, T], F32, name="h")
-            if i < PACK:
-                cols = slice(i % 2 * P, (i % 2 + 1) * P)
-                codes = [w_codes[i // 2][:, c, cols] for c in range(C)]
-                scales = [w_scales[i // 2][:, c, cols] for c in range(C)]
+        def project(b, parts=1):
+            acc = psum_h.tile([P, T], F32, name="acc_h")
+            h[b] = four.tile([P, T], F32, name="h")
+            if b < PACK:
+                codes, scales = lower_codes[b // 2], lower_scales[b // 2]
+                columns = slice(b % 2 * P, (b % 2 + 1) * P)
             else:
-                cols = slice((i - PACK) * P, (i - PACK + 1) * P)
-                codes = [big_codes[:, c, cols] for c in range(C)]
-                scales = [big_scales[:, c, cols] for c in range(C)]
-            width = T // parts
+                codes, scales = upper_codes, upper_scales
+                columns = slice((b - PACK) * P, (b - PACK + 1) * P)
             for part in range(parts):
-                nodes = slice(part * width, (part + 1) * width)
-                for c in range(C):
+                nodes = slice(part * T // parts, (part + 1) * T // parts)
+                for c in range(K_PASSES):
                     nc.tensor.matmul_mx(
                         out=acc[:, nodes],
-                        lhsT=codes[c].bitcast(FP8X4),
-                        lhsT_scale=scales[c],
+                        lhsT=codes[:, c, columns].bitcast(FP8X4),
+                        lhsT_scale=scales[:, c, columns],
                         rhs=x_codes[:, c, nodes].bitcast(FP8X4),
                         rhs_scale=x_scales[:, c, nodes],
                         start=(c == 0),
-                        stop=(c == C - 1),
+                        stop=(c == K_PASSES - 1),
                     )
-                nc.scalar.activation(h[:, nodes], acc[:, nodes], GELU)
-            return h
+                nc.scalar.activation(h[b][:, nodes], acc[:, nodes], GELU)
 
-        zT = [held.tile([P, Q, PACK, P], F32, name=f"zT{half}") for half in range(2)]
-        z_codes = held.tile([P, Q, V], U32, align_bytes=64)
-        z_scales = held.tile([P, Q, V], U8, align_bytes=64)
-        z_g = [held.tile([P, V, PACK], BF16, name=f"z_g{q}", align_bytes=64) for q in range(Q)]
+        z_targets = [held.tile([P, I_PASSES, PACK, P], F32, name=f"z_targets{half}") for half in range(2)]
+        z_grouped = [held.tile([P, V, PACK], BF16, name=f"z_grouped{q}", align_bytes=64) for q in range(I_PASSES)]
+        z_codes = held.tile([P, I_PASSES, V], U32, align_bytes=64)
+        z_scales = held.tile([P, I_PASSES, V], U8, align_bytes=64)
+        late = held.tile([P, 2, V], F32)
+        turned = {}
 
-        def gather(out, h, d):
-            nc.vector.tensor_tensor(out, h[:].indirect(lists[d][:]), gates[:, d], MULT)
+        def targets(half):
+            return slice(half * HALF, (half + 1) * HALF)
 
-        def add_up(i, prods):
-            for half in range(2):
-                accs[half] = ps_z.tile([P, P], F32, name=f"acc_z{half}")
-            for d, prod in enumerate(prods):
+        def sum_block(b, products):
+            q, t = divmod(b, PACK)
+            sums = [psum_z.tile([P, P], F32, name=f"sum{half}") for half in range(2)]
+            for d, product in enumerate(products):
                 for half in range(2):
                     nc.tensor.matmul(
-                        accs[half][:],
-                        lhsT=prod[:, half * HALF : (half + 1) * HALF],
-                        rhs=ident[:],
+                        sums[half][:],
+                        lhsT=product[:, targets(half)],
+                        rhs=identity[:],
                         start=(d == 0),
-                        stop=(d == len(prods) - 1),
+                        stop=(d == len(products) - 1),
                         is_transpose=True,
                     )
             for half in range(2):
-                keep_sum(nc.scalar.copy, i, half, accs[half])
+                if q == 0:
+                    kept = z_targets[half][:, q, :, 32 * b : 32 * (b + 1)]
+                    nc.scalar.copy(out=kept, in_=sums[half][:].rearrange("p (m u) -> p u m", u=PACK))
+                else:
+                    nc.scalar.copy(out=z_targets[half][:, q, t], in_=sums[half][:])
 
-        def keep_sum(copy, i, half, acc):
-            q, b = divmod(i, PACK)
-            if q == 0:
-                copy(
-                    out=zT[half][:, 0, :, 32 * b : 32 * (b + 1)],
-                    in_=acc[:].rearrange("p (m t) -> p t m", t=PACK),
-                )
-            else:
-                copy(out=zT[half][:, 1, b], in_=acc[:])
+        def turn_back(q, half, slots):
+            for t in slots:
+                nc.tensor.transpose(turned[half][:, t], z_targets[half][:, q, t], identity[:])
 
-        def interleave_z(copy, q, half, back, planes):
-            v = slice(half * HALF, (half + 1) * HALF)
-            copy(out=z_g[q][:, v, planes], in_=back[:, planes].rearrange("p t v -> p v t"))
-
-        accs = [None, None]
-        backs = [None, None]
-
-        def quantize_z(q, v0=0, width=V):
-            nc.vector.quantize_mx(
-                out=z_codes[:, q, v0 : v0 + width].bitcast(FP8X4),
-                scales=z_scales[:, q, v0 : v0 + width],
-                in_=z_g[q][:, v0 : v0 + width].rearrange("p v t -> p (v t)"),
+        def round_turned(q, half, slots):
+            nc.scalar.copy(
+                out=z_grouped[q][:, targets(half), slots],
+                in_=turned[half][:, slots].rearrange("p t v -> p v t"),
             )
 
-        hs = {0: project(0, parts=2)}
-        n_tiles = H // P
-        w2_codes = held.tile([P, Q, N], U32, align_bytes=64)
-        w2_scales = held.tile([P, Q, N], U8, align_bytes=64)
-        late = held.tile([P, 2, V], F32)
-        prods = []
-        seq = [(i, d) for i in range(n_tiles) for d in range(D) if not (i >= 6 and d == D - 1)] + [(6, D - 1), (7, D - 1)]
-        for slot in range(48):
-                i, d = seq[slot]
-                if slot in QUANT_SLOTS:
-                    quantize_w(1, QUANT_SLOTS.index(slot))
-                for c in range(C):
-                    if slot == BIG_SLOTS[c]:
-                        quantize_big(c)
-                if slot in PROJECT_SLOTS:
-                    n = PROJECT_SLOTS.index(slot) + 1
-                    hs[n] = project(n)
-                if slot == Z_SLOT:
-                    quantize_z(0)
-                if slot == W2_SLOT:
-                    nc.vector.quantize_mx(
-                        out=w2_codes[:].rearrange("p q m -> p (q m)").bitcast(FP8X4),
-                        scales=w2_scales[:].rearrange("p q m -> p (q m)"),
-                        in_=groups["w2"][:].rearrange("p q m j -> p (q m j)"),
-                    )
-                if slot >= 46:
-                    gather(late[:, i - 6], hs[i], d)
-                else:
-                    if slot == QUANT_SLOTS[1]:
-                        prod = held.tile([P, V], F32, name="group_w1", align_bytes=64)
-                    elif slot == BIG_SLOTS[3]:
-                        prod = held.tile([P, V], F32, name="group_big3", align_bytes=64)
-                    else:
-                        prod = stage.tile([P, V], F32, name=f"prod{d}")
-                    gather(prod[:], hs[i], d)
-                    prods.append(prod)
-                if slot in TOKEN_SLOTS:
-                    token = stage.tile([P, 1], F32, name="token")
-                    nc.scalar.activation(token[:], prod[:, :1], COPY, bias=1.0, scale=0.0)
+        def quantize_z(q, v):
+            quantize(z_codes[:, q, v], z_scales[:, q, v], z_grouped[q][:, v].rearrange("p v t -> p (v t)"))
 
-                    def copy(out, in_):
-                        nc.scalar.activation(out, in_, COPY, scale=token[:])
+        before = {
+            0: [lambda: project(1)],
+            6: [lambda: quantize_lower(1, 0)],
+            9: [lambda: quantize_lower(1, 1), lambda: project(2)],
+            10: [lambda: project(3)],
+            12: [lambda: quantize_upper(0)],
+            16: [lambda: quantize_upper(1)],
+            19: [lambda: quantize_upper(2)],
+            21: [lambda: quantize_upper(3), lambda: project(4)],
+            29: [lambda: project(5)],
+            30: [lambda: project(6), lambda: quantize_z(0, slice(0, V))],
+            34: [lambda: project(7)],
+            43: [quantize_w2],
+        }
+        behind = {
+            0: [lambda: copy_lower(1)],
+            7: [lambda: copy_upper(0)],
+            9: [lambda: copy_upper(1)],
+            12: [lambda: copy_upper(2)],
+            17: [lambda: copy_upper(3)],
+            19: [copy_w2],
+        }
+        takes_buffer_of = {9: "lower_grouped1", 21: "upper_grouped3"}
 
-                    n = TOKEN_SLOTS.index(slot)
-                    if n == 0:
-                        for c in range(C):
-                            copy_w(copy, 1, c)
-                    elif n < 5:
-                        for part in range(2):
-                            copy_big(copy, n - 1, part)
-                    else:
-                        groups["w2"] = stage.tile([P, Q, N, PACK], BF16, name="grouped", align_bytes=64)
-                        for q in range(Q):
-                            interleave(copy, groups["w2"][:, q], w2_raw[:, q])
-                if (i < 6 and d == D - 1) or (i >= 6 and d == D - 2):
-                    add_up(i, prods)
-                    prods = []
-                    if i % PACK == 0:
+        project(0, parts=2)
+        products = []
+        for place, (b, d) in enumerate(GATHERS):
+            for step in before.get(place, []):
+                step()
+            if place >= LATE:
+                product = late[:, place - LATE]
+            elif place in takes_buffer_of:
+                product = held.tile([P, V], F32, name=takes_buffer_of[place], align_bytes=64)[:]
+            else:
+                product = two.tile([P, V], F32, name=f"product{d}")[:]
+            nc.vector.tensor_tensor(product, h[b][:].indirect(lists[d][:]), gates[:, d], MULT)
+            products.append(product)
+            for step in behind.get(place, []):
+                step()
+
+            if place < LATE and (place + 1 == LATE or GATHERS[place + 1][0] != b):
+                q, t = divmod(b, PACK)
+                sum_block(b, products)
+                products = []
+                if t == 0:
+                    for half in range(2):
+                        turned[half] = psum_z.tile([P, PACK, HALF], F32, name=f"turned{half}")
+                if q == 0 and t == PACK - 1:
+                    for half in range(2):
+                        turn_back(0, half, range(PACK))
+                        round_turned(0, half, slice(0, PACK))
+                if q == 1:
+                    for half in range(2):
+                        turn_back(1, half, [t])
+                    if t == 1:
                         for half in range(2):
-                            backs[half] = ps_z.tile([P, PACK, HALF], F32, name=f"back{half}")
-                    if i == PACK - 1:
-                        for half in range(2):
-                            for t in range(PACK):
-                                nc.tensor.transpose(backs[half][:, t], zT[half][:, 0, t], ident[:])
-                            interleave_z(nc.scalar.copy, 0, half, backs[half], slice(0, PACK))
-                    if i >= PACK:
-                        for half in range(2):
-                            nc.tensor.transpose(backs[half][:, i - PACK], zT[half][:, 1, i - PACK], ident[:])
-                    if i == 5:
-                        for half in range(2):
-                            interleave_z(nc.scalar.copy, 1, half, backs[half], slice(0, 2))
+                            round_turned(1, half, slice(0, 2))
+
         for half in range(2):
-            v = slice(half * HALF, (half + 1) * HALF)
             nc.vector.tensor_tensor(
-                z_g[1][:, v, 2:4],
-                backs[half][:, 2:4].rearrange("p t v -> p v t"),
-                late[:, :, v].rearrange("p t v -> p v t"),
+                z_grouped[1][:, targets(half), 2:4],
+                turned[half][:, 2:4].rearrange("p t v -> p v t"),
+                late[:, :, targets(half)].rearrange("p t v -> p v t"),
                 ADD,
             )
-        quantize_z(1)
-        for b in range(N // P):
-            acc = ps_z.tile([P, V], F32, name=f"acc_o{b}")
-            for q in range(Q):
-                nc.tensor.matmul_mx(
-                    out=acc[:],
-                    lhsT=w2_codes[:, q, b * P : (b + 1) * P].bitcast(FP8X4),
-                    lhsT_scale=w2_scales[:, q, b * P : (b + 1) * P],
-                    rhs=z_codes[:, q].bitcast(FP8X4),
-                    rhs_scale=z_scales[:, q],
-                    start=(q == 0),
-                    stop=(q == Q - 1),
-                )
-            res = held.tile([P, V], F32, name=f"res{b}")
-            if b:
-                nc.scalar.copy(out=res[:], in_=acc[:])
-            else:
-                nc.vector.tensor_copy(out=res[:], in_=acc[:])
-            nc.sync.dma_start(out=out[b * P : (b + 1) * P, :], in_=res[:])
+        for half in range(2):
+            quantize_z(1, targets(half))
+
+        for half in range(2):
+            acc = psum_z.tile([P, N // P, HALF], F32, name=f"acc_out{half}")
+            for m in range(N // P):
+                columns = slice(m * P, (m + 1) * P)
+                for q in range(I_PASSES):
+                    nc.tensor.matmul_mx(
+                        out=acc[:, m],
+                        lhsT=w2_codes[:, q, columns].bitcast(FP8X4),
+                        lhsT_scale=w2_scales[:, q, columns],
+                        rhs=z_codes[:, q, targets(half)].bitcast(FP8X4),
+                        rhs_scale=z_scales[:, q, targets(half)],
+                        start=(q == 0),
+                        stop=(q == I_PASSES - 1),
+                    )
+            result = held.tile([P, N // P, HALF], F32, name=f"result{half}")
+            copy = nc.vector.tensor_copy if half else nc.scalar.copy
+            copy(out=result[:], in_=acc[:])
+            nc.sync.dma_start(out=out[:, targets(half)].rearrange("(m p) v -> p m v", p=P), in_=result[:])

import concourse.mybir as mybir
from concourse.masks import make_identity

K, T, D, V, H, N = 2048, 512, 6, 256, 1024, 256

F32 = mybir.dt.float32
BF16 = mybir.dt.bfloat16
U32 = mybir.dt.uint32
U16 = mybir.dt.uint16
U8 = mybir.dt.uint8
FP8X4 = mybir.dt.float8_e4m3fn_x4
MULT = mybir.AluOpType.mult
ADD = mybir.AluOpType.add
GELU = mybir.ActivationFunctionType.Gelu_apprx_tanh

FLOPS = 2 * K * H * T + 2 * D * H * V + 2 * H * N * V

P = 128
PACK = 4
PASS = P * PACK
K_PASSES = K // PASS
I_PASSES = H // PASS
BLOCKS = H // P
CHUNK = 256
HALF = V // 2

X_PIECES = ((0, 0, T), (1, 0, T), (2, 0, T), (3, 0, T // 2), (3, T // 2, T // 2))
VECTOR_SHARE = 11

GATHERS = [(b, d) for b in range(BLOCKS) for d in range(D) if b < BLOCKS - 2 or d < D - 1] + [
    (b, D - 1) for b in (BLOCKS - 2, BLOCKS - 1)
]
LATE = len(GATHERS) - 2


def tile_picked_gcn_mlp_gelu_sub_l_kernel(
    tc, xT, w1, w2, gate, pos1, pos2, pos3, pos4, pos5, pos6, out
):
    nc = tc.nc
    with (
        tc.tile_pool(name="held", bufs=1) as held,
        tc.tile_pool(name="four", bufs=4) as four,
        tc.tile_pool(name="two", bufs=2) as two,
        tc.psum_pool(name="psum_h", bufs=2) as psum_h,
        tc.psum_pool(name="psum_z", bufs=1) as psum_z,
    ):
        zero = held.tile([P, 1], F32)
        unused = held.tile([P, 1], F32)
        nc.vector.memset(zero[:], 0.0)
        nc.scalar.activation(unused[:], zero[:], GELU)
        identity = held.tile([P, P], F32)
        make_identity(nc, identity[:])

        def rows_of_pass(matrix, c, columns):
            return matrix[c * PASS : (c + 1) * PASS, columns].rearrange("(p j) w -> p j w", j=PACK)

        lower_raw = []

        def load_lower(n):
            raw = two.tile([P, K_PASSES, PACK, CHUNK], F32, name="lower_raw")
            for c in range(K_PASSES):
                nc.sync.dma_start(out=raw[:, c], in_=rows_of_pass(w1, c, slice(n * CHUNK, (n + 1) * CHUNK)))
            lower_raw.append(raw)

        load_lower(0)
        x_raw = []
        lists = []
        for n, (c, t0, nodes) in enumerate(X_PIECES):
            raw = four.tile([P, PACK, nodes], F32, name="raw" if nodes == T else f"x_raw{t0}")
            nc.sync.dma_start(out=raw[:], in_=rows_of_pass(xT, c, slice(t0, t0 + nodes)))
            x_raw.append(raw)
            if n == 1:
                for d, pos in enumerate((pos1, pos2, pos3, pos4, pos5, pos6)):
                    offsets = held.tile([P, V // 16], U16, name=f"offsets{d}")
                    nc.sync.dma_start(offsets[:], pos)
                    lists.append(offsets)
        gates = held.tile([P, D, V], F32)
        nc.sync.dma_start(out=gates[:], in_=gate.rearrange("d p v -> p d v"))
        load_lower(1)
        upper_raw = []
        for c in range(K_PASSES):
            raw = four.tile([P, PACK, PASS], F32, name="raw")
            nc.sync.dma_start(out=raw[:], in_=rows_of_pass(w1, c, slice(PASS, H)))
            upper_raw.append(raw)
        w2_raw = held.tile([P, I_PASSES, PACK, N], F32)
        nc.sync.dma_start(out=w2_raw[:], in_=w2.rearrange("(q p j) m -> p q j m", q=I_PASSES, j=PACK))

        def interleave(copy, grouped, raw):
            copy(
                out=grouped.rearrange("p (c i) j -> p c j i", i=4),
                in_=raw.rearrange("p j (c i) -> p c j i", i=4),
            )

        def quantize(codes, scales, grouped):
            nc.vector.quantize_mx(out=codes.bitcast(FP8X4), scales=scales, in_=grouped)

        lower_codes = [held.tile([P, K_PASSES, CHUNK], U32, name=f"lower_codes{n}", align_bytes=64) for n in range(2)]
        lower_scales = [held.tile([P, K_PASSES, CHUNK], U8, name=f"lower_scales{n}", align_bytes=64) for n in range(2)]
        lower_grouped = {}

        def copy_lower(n):
            lower_grouped[n] = held.tile([P, K_PASSES, CHUNK, PACK], BF16, name=f"lower_grouped{n}", align_bytes=64)
            for c in range(K_PASSES):
                interleave(nc.scalar.copy, lower_grouped[n][:, c], lower_raw[n][:, c])

        def quantize_lower(n, s):
            passes = slice(2 * s, 2 * s + 2)
            quantize(
                lower_codes[n][:, passes].rearrange("p c w -> p (c w)"),
                lower_scales[n][:, passes].rearrange("p c w -> p (c w)"),
                lower_grouped[n][:, passes].rearrange("p c w j -> p (c w j)"),
            )

        upper_codes = held.tile([P, K_PASSES, PASS], U32, align_bytes=64)
        upper_scales = held.tile([P, K_PASSES, PASS], U8, align_bytes=64)
        upper_grouped = {}

        def copy_upper(c):
            upper_grouped[c] = held.tile([P, PACK, P, PACK], BF16, name=f"upper_grouped{c}", align_bytes=64)
            for half in range(2):
                m = slice(half * P // 2, (half + 1) * P // 2)
                columns = slice(half * PASS // 2, (half + 1) * PASS // 2)
                nc.scalar.copy(
                    out=upper_grouped[c][:, :, m].rearrange("p t m j -> p m j t"),
                    in_=upper_raw[c][:, :, columns].rearrange("p j (m t) -> p m j t", t=PACK),
                )

        def quantize_upper(c):
            quantize(upper_codes[:, c], upper_scales[:, c], upper_grouped[c][:].rearrange("p t m j -> p (t m j)"))

        w2_codes = held.tile([P, I_PASSES, N], U32, align_bytes=64)
        w2_scales = held.tile([P, I_PASSES, N], U8, align_bytes=64)
        w2_grouped = held.tile([P, I_PASSES, N, PACK], BF16, align_bytes=64)

        def copy_w2():
            for q in range(I_PASSES):
                interleave(nc.scalar.copy, w2_grouped[:, q], w2_raw[:, q])

        def quantize_w2():
            quantize(
                w2_codes[:].rearrange("p q m -> p (q m)"),
                w2_scales[:].rearrange("p q m -> p (q m)"),
                w2_grouped[:].rearrange("p q m j -> p (q m j)"),
            )

        copy_lower(0)
        for s in range(2):
            quantize_lower(0, s)
        x_codes = held.tile([P, K_PASSES, T], U32, align_bytes=64)
        x_scales = held.tile([P, K_PASSES, T], U8, align_bytes=64)
        for n, (c, t0, nodes) in enumerate(X_PIECES):
            cut = nodes * VECTOR_SHARE // 16
            x_grouped = held.tile([P, nodes, PACK], BF16, name=f"x_grouped{n}", align_bytes=64)
            interleave(nc.vector.tensor_copy, x_grouped[:, :cut], x_raw[n][:, :, :cut])
            interleave(nc.scalar.copy, x_grouped[:, cut:], x_raw[n][:, :, cut:])
            quantize(
                x_codes[:, c, t0 : t0 + nodes],
                x_scales[:, c, t0 : t0 + nodes],
                x_grouped[:].rearrange("p t j -> p (t j)"),
            )

        h = {}

        def project(b, parts=1):
            acc = psum_h.tile([P, T], F32, name="acc_h")
            h[b] = four.tile([P, T], F32, name="h")
            if b < PACK:
                codes, scales = lower_codes[b // 2], lower_scales[b // 2]
                columns = slice(b % 2 * P, (b % 2 + 1) * P)
            else:
                codes, scales = upper_codes, upper_scales
                columns = slice((b - PACK) * P, (b - PACK + 1) * P)
            for part in range(parts):
                nodes = slice(part * T // parts, (part + 1) * T // parts)
                for c in range(K_PASSES):
                    nc.tensor.matmul_mx(
                        out=acc[:, nodes],
                        lhsT=codes[:, c, columns].bitcast(FP8X4),
                        lhsT_scale=scales[:, c, columns],
                        rhs=x_codes[:, c, nodes].bitcast(FP8X4),
                        rhs_scale=x_scales[:, c, nodes],
                        start=(c == 0),
                        stop=(c == K_PASSES - 1),
                    )
                nc.scalar.activation(h[b][:, nodes], acc[:, nodes], GELU)

        z_targets = [held.tile([P, I_PASSES, PACK, P], F32, name=f"z_targets{half}") for half in range(2)]
        z_grouped = [held.tile([P, V, PACK], BF16, name=f"z_grouped{q}", align_bytes=64) for q in range(I_PASSES)]
        z_codes = held.tile([P, I_PASSES, V], U32, align_bytes=64)
        z_scales = held.tile([P, I_PASSES, V], U8, align_bytes=64)
        late = held.tile([P, 2, V], F32)
        turned = {}

        def targets(half):
            return slice(half * HALF, (half + 1) * HALF)

        def sum_block(b, products):
            q, t = divmod(b, PACK)
            sums = [psum_z.tile([P, P], F32, name=f"sum{half}") for half in range(2)]
            for d, product in enumerate(products):
                for half in range(2):
                    nc.tensor.matmul(
                        sums[half][:],
                        lhsT=product[:, targets(half)],
                        rhs=identity[:],
                        start=(d == 0),
                        stop=(d == len(products) - 1),
                        is_transpose=True,
                    )
            for half in range(2):
                if q == 0:
                    kept = z_targets[half][:, q, :, 32 * b : 32 * (b + 1)]
                    nc.scalar.copy(out=kept, in_=sums[half][:].rearrange("p (m u) -> p u m", u=PACK))
                else:
                    nc.scalar.copy(out=z_targets[half][:, q, t], in_=sums[half][:])

        def turn_back(q, half, slots):
            for t in slots:
                nc.tensor.transpose(turned[half][:, t], z_targets[half][:, q, t], identity[:])

        def round_turned(q, half, slots):
            nc.scalar.copy(
                out=z_grouped[q][:, targets(half), slots],
                in_=turned[half][:, slots].rearrange("p t v -> p v t"),
            )

        def quantize_z(q, v):
            quantize(z_codes[:, q, v], z_scales[:, q, v], z_grouped[q][:, v].rearrange("p v t -> p (v t)"))

        before = {
            0: [lambda: project(1)],
            6: [lambda: quantize_lower(1, 0)],
            9: [lambda: quantize_lower(1, 1), lambda: project(2)],
            10: [lambda: project(3)],
            12: [lambda: quantize_upper(0)],
            16: [lambda: quantize_upper(1)],
            19: [lambda: quantize_upper(2)],
            21: [lambda: quantize_upper(3), lambda: project(4)],
            29: [lambda: project(5)],
            30: [lambda: project(6), lambda: quantize_z(0, slice(0, V))],
            34: [lambda: project(7)],
            43: [quantize_w2],
        }
        behind = {
            0: [lambda: copy_lower(1)],
            7: [lambda: copy_upper(0)],
            9: [lambda: copy_upper(1)],
            12: [lambda: copy_upper(2)],
            17: [lambda: copy_upper(3)],
            19: [copy_w2],
        }
        takes_buffer_of = {9: "lower_grouped1", 21: "upper_grouped3"}

        project(0, parts=2)
        products = []
        for place, (b, d) in enumerate(GATHERS):
            for step in before.get(place, []):
                step()
            if place >= LATE:
                product = late[:, place - LATE]
            elif place in takes_buffer_of:
                product = held.tile([P, V], F32, name=takes_buffer_of[place], align_bytes=64)[:]
            else:
                product = two.tile([P, V], F32, name=f"product{d}")[:]
            nc.vector.tensor_tensor(product, h[b][:].indirect(lists[d][:]), gates[:, d], MULT)
            products.append(product)
            for step in behind.get(place, []):
                step()

            if place < LATE and (place + 1 == LATE or GATHERS[place + 1][0] != b):
                q, t = divmod(b, PACK)
                sum_block(b, products)
                products = []
                if t == 0:
                    for half in range(2):
                        turned[half] = psum_z.tile([P, PACK, HALF], F32, name=f"turned{half}")
                if q == 0 and t == PACK - 1:
                    for half in range(2):
                        turn_back(0, half, range(PACK))
                        round_turned(0, half, slice(0, PACK))
                if q == 1:
                    for half in range(2):
                        turn_back(1, half, [t])
                    if t == 1:
                        for half in range(2):
                            round_turned(1, half, slice(0, 2))

        for half in range(2):
            nc.vector.tensor_tensor(
                z_grouped[1][:, targets(half), 2:4],
                turned[half][:, 2:4].rearrange("p t v -> p v t"),
                late[:, :, targets(half)].rearrange("p t v -> p v t"),
                ADD,
            )
        for half in range(2):
            quantize_z(1, targets(half))

        for half in range(2):
            acc = psum_z.tile([P, N // P, HALF], F32, name=f"acc_out{half}")
            for m in range(N // P):
                columns = slice(m * P, (m + 1) * P)
                for q in range(I_PASSES):
                    nc.tensor.matmul_mx(
                        out=acc[:, m],
                        lhsT=w2_codes[:, q, columns].bitcast(FP8X4),
                        lhsT_scale=w2_scales[:, q, columns],
                        rhs=z_codes[:, q, targets(half)].bitcast(FP8X4),
                        rhs_scale=z_scales[:, q, targets(half)],
                        start=(q == 0),
                        stop=(q == I_PASSES - 1),
                    )
            result = held.tile([P, N // P, HALF], F32, name=f"result{half}")
            copy = nc.vector.tensor_copy if half else nc.scalar.copy
            copy(out=result[:], in_=acc[:])
            nc.sync.dma_start(out=out[:, targets(half)].rearrange("(m p) v -> p m v", p=P), in_=result[:])
